import numpy as np
import ml_dtypes


def mxq(x, axis, fmt="e4m3"):
    dtype, down = {"e4m3": (ml_dtypes.float8_e4m3fn, 7), "e5m2": (ml_dtypes.float8_e5m2, 14)}[fmt]
    v = np.moveaxis(np.asarray(x, np.float32).astype(ml_dtypes.bfloat16).astype(np.float64), axis, -1)
    blocks = v.reshape(v.shape[:-1] + (-1, 32))
    amax = np.abs(blocks).max(-1, keepdims=True)
    byte = np.maximum(np.where(amax > 0, np.frexp(amax)[1] - 1 + 127, 0) - down, 1)
    scale = np.exp2(byte - 127.0)
    codes = (blocks / scale).astype(np.float32).astype(dtype).astype(np.float64)
    return np.moveaxis((codes * scale).reshape(v.shape), -1, axis)


WIDE = False


def mx_kscale(k):
    if not WIDE:
        return np.ones(k)
    levels = np.array([10, -10, 5, -5, 0])
    if k % 512:
        return np.exp2(np.random.permutation(np.resize(levels, k // 32))).repeat(32)
    a = np.empty((k // 512, 16))
    for p in range(k // 512):
        a[p, :8] = np.random.permutation(np.resize(levels, 8))
        for g in range(8):
            far = levels[np.abs(levels - a[p, g]) >= 10]
            a[p, g + 8] = far[np.random.randint(len(far))]
    return np.exp2(a.ravel()).repeat(32)


BF16 = ml_dtypes.bfloat16


def bf(x):
    return np.asarray(x, np.float32).astype(BF16)


def f64(x):
    return np.asarray(x).astype(np.float64)


E2M1 = np.array([0.0, 0.5, 1.0, 1.5, 2.0, 3.0, 4.0, 6.0, -0.0, -0.5, -1.0, -1.5, -2.0, -3.0, -4.0, -6.0])


def pack_weight(w, fmt):
    k, n = w.shape
    w = f64(bf(w)).reshape(k // 32, 32, n)
    amax = np.abs(w).max(1)
    if fmt == "e4m3":
        byte = np.frexp(amax)[1] - 1 + 127 - 7
    else:
        mant, ex = np.frexp(amax / 6.0)
        byte = np.where(mant > 0.5, ex, ex - 1) + 127
    byte = np.clip(np.where(amax > 0, byte, 1), 1, 254)
    scaled = (w * np.exp2(127.0 - byte)[:, None, :]).reshape(k, n).astype(np.float32)
    by_word = np.ascontiguousarray(scaled.reshape(k // 512, 128, 4, n).transpose(0, 1, 3, 2))
    if fmt == "e4m3":
        words = by_word.astype(ml_dtypes.float8_e4m3fn).view(np.uint8)
    else:
        c = by_word.astype(ml_dtypes.float4_e2m1fn).view(np.uint8) & 0xF
        words = c[..., 0::2] | (c[..., 1::2] << 4)
    return np.ascontiguousarray(words), np.ascontiguousarray(byte.astype(np.uint8).reshape(k // 512, 16, n))


def unpack_weight(words, scales, fmt):
    g, p, n, _ = words.shape
    if fmt == "e4m3":
        vals = np.ascontiguousarray(words).view(ml_dtypes.float8_e4m3fn).astype(np.float64)
    else:
        nib = np.empty((g, p, n, 4), np.uint8)
        nib[..., 0::2] = words & 0xF
        nib[..., 1::2] = words >> 4
        vals = E2M1[nib]
    vals = vals * np.repeat(np.exp2(scales.astype(np.float64) - 127.0), 8, axis=1)[..., None]
    return vals.transpose(0, 1, 3, 2).reshape(g * 512, n)
def pack4(w):
    words, scales = pack_weight(w, "e2m1")
    return words.reshape(words.shape[0], 128, -1), scales


def unpack4(words, scales):
    return unpack_weight(words.reshape(words.shape[0], 128, -1, 2), scales, "e2m1")


M, K, L, N = 1024, 2048, 512, 1536

DUR_MIN, DUR_RANGE = 1.0, 4.0
SPREAD_MIN, SPREAD_RANGE = 0.02, 0.28
STRESS_RANGE = 0.8


def setup_inputs():
    s, t = mx_kscale(K), mx_kscale(L)
    x = np.random.standard_normal((M, K)) * s
    y = np.random.standard_normal((M, L)) * t
    base = np.random.standard_normal((K, N)) / np.sqrt(K) / s[:, None]
    distressed = np.random.standard_normal((L, N)) / np.sqrt(L) / t[:, None]
    base_words, base_scales = pack4(base)
    return {"x": bf(x),
            "y": bf(y),
            "stress": bf(1 + STRESS_RANGE * np.random.random(L)),
            "base_words": base_words,
            "base_scales": base_scales,
            "distressed": bf(distressed),
            "duration": bf(DUR_MIN + DUR_RANGE * np.random.random(M)),
            "spread": bf(SPREAD_MIN + SPREAD_RANGE * np.random.random(N))}


def reference(x, y, stress, base_words, base_scales, distressed, duration, spread):
    ys = f64(y) * f64(stress)
    h = ((mxq(f64(x), 1, "e4m3") @ unpack4(base_words, base_scales))
         + (mxq(ys, 1, "e4m3") @ mxq(f64(distressed), 0, "e4m3")))
    discount = np.exp(-f64(duration)[:, None] * f64(spread)[None, :])
    return h * discount

@@ -1,0 +1,384 @@
+from contextlib import ExitStack
+
+import concourse.mybir as mybir
+from concourse.masks import make_identity
+
+M, K, L, N = 1024, 2048, 512, 1536
+FLOPS = 2 * M * (K + L) * N
+
+F32 = mybir.dt.float32
+BF16 = mybir.dt.bfloat16
+U32 = mybir.dt.uint32
+I32 = mybir.dt.int32
+U8 = mybir.dt.uint8
+FP8X4 = mybir.dt.float8_e4m3fn_x4
+FP4X4 = mybir.dt.float4_e2m1fn_x4
+ACT = mybir.ActivationFunctionType
+MULT = mybir.AluOpType.mult
+
+P = 128
+TILES = M // P
+G = K // 512
+NB = 512
+NN = N // NB
+
+
+def tile_stressed_rating_migration_s1_kernel(
+    tc, x, y, stress, base_words, base_scales, distressed, duration, spread, out
+):
+    nc = tc.nc
+    with ExitStack() as ctx:
+        keep = ctx.enter_context(tc.tile_pool(name="keep", bufs=1))
+        work = ctx.enter_context(tc.tile_pool(name="work", bufs=3))
+        psum = ctx.enter_context(tc.psum_pool(name="psum", bufs=1))
+
+        x_view = x.rearrange("(p i) k -> p i k", i=TILES)
+        y_view = y.rearrange("(p i) l -> p i l", i=TILES)
+        out_view = out.rearrange("(p i) n -> p i n", i=TILES)
+
+        def bank(b, shape, dtype):
+            t = psum.tile(shape, dtype, name=f"bank{b}", tag=f"bank{b}")
+            return t
+
+        x_raw = []
+        for i in range(TILES):
+            t = keep.tile([P, K], BF16, name=f"x_raw{i}", align_bytes=64)
+            x_raw.append(t)
+        y_raw = keep.tile([P, TILES, L], BF16, name="y_raw", align_bytes=64)
+        words = keep.tile([P, G, 2 * N], U8, name="words", align_bytes=64)
+        scales_a = keep.tile([P, 2, N], U8, name="scales_a", align_bytes=64)
+        scales_b = keep.tile([P, 2, N], U8, name="scales_b", align_bytes=64)
+        scales = [scales_a[:, 0, :], scales_a[:, 1, :], scales_b[:, 0, :], scales_b[:, 1, :]]
+        d_raw, d_grouped, d_codes, d_scales = [], [], [], []
+        for n in range(NN):
+            t = keep.tile([P, 4, NB], BF16, name=f"d_raw{n}", align_bytes=64)
+            d_raw.append(t)
+            t = keep.tile([P, NB, 4], BF16, name=f"d_grouped{n}", align_bytes=64)
+            d_grouped.append(t)
+            t = keep.tile([P, NB], U32, name=f"d_codes{n}", align_bytes=64)
+            d_codes.append(t)
+            t = keep.tile([P, NB], U8, name=f"d_scales{n}", align_bytes=64)
+            d_scales.append(t)
+        spread_col = keep.tile([P, 2, 6], BF16, name="spread_col")
+        spread_row = keep.tile([P, N], BF16, name="spread_row")
+        stress_col = keep.tile([P, 4], BF16, name="stress_col")
+        dur_raw = keep.tile([P, TILES], BF16, name="dur_raw")
+        neg_dur = keep.tile([P, TILES], F32, name="neg_dur")
+        ident_f = keep.tile([P, P], F32, name="ident_f")
+        ident_b = keep.tile([P, P], BF16, name="ident_b")
+        warm = keep.tile([P, 1], F32, name="warm")
+
+        def load_x(i, part, parts):
+            w = K // parts
+            nc.sync.dma_start(
+                out=x_raw[i][:, part * w : (part + 1) * w],
+                in_=x_view[:, i, part * w : (part + 1) * w],
+            )
+
+        def load_y(i0, i1):
+            nc.sync.dma_start(out=y_raw[:, i0:i1, :], in_=y_view[:, i0:i1, :])
+
+        def load_words(g):
+            nc.sync.dma_start(out=words[:, g, :].bitcast(I32), in_=base_words[g].bitcast(I32))
+
+        def load_scales(t, g0, g1):
+            for q in range(4):
+                nc.sync.dma_start(
+                    out=t[32 * q : 32 * q + 4, :, :].bitcast(I32),
+                    in_=base_scales[g0:g1, 4 * q : 4 * q + 4, :].rearrange("g r n -> r g n").bitcast(I32),
+                )
+
+        def load_d(n):
+            d_view = distressed.rearrange("(p j) n -> p j n", j=4)
+            nc.sync.dma_start(out=d_raw[n][:], in_=d_view[:, :, n * NB : (n + 1) * NB])
+
+        x_perm, x_group, x_codes, x_scales = {}, {}, {}, {}
+        y_group, y_codes, y_scales = {}, {}, {}
+
+        def permute_x(i):
+            t = work.tile([P, 2, K // 4], F32, name="x_perm", align_bytes=64)
+            nc.vector.tensor_copy(
+                out=t[:], in_=x_raw[i][:].bitcast(F32).rearrange("p (w u) -> p u w", u=2)
+            )
+            x_perm[i] = t
+
+        def transpose_x(i, half, b):
+            t = bank(b, [P, 4, P], F32)
+            for s in range(4):
+                g, u = 2 * half + s // 2, s % 2
+                if i in x_perm:
+                    src = x_perm[i][:, u, P * g : P * (g + 1)]
+                else:
+                    src = x_raw[i][:].bitcast(F32)[:, 256 * g + u : 256 * (g + 1) : 2]
+                nc.tensor.transpose(t[:, s, :], src, ident_f[:])
+            return t
+
+        def copy_x(i, half, t, eng):
+            if i not in x_group:
+                gt = work.tile([P, G, P, 4], BF16, name="x_group", align_bytes=64)
+                x_group[i] = gt
+            dst = x_group[i][:, 2 * half : 2 * half + 2, :, :].rearrange("p g m t -> p (g m t)")
+            dst = dst.bitcast(F32).rearrange("p (g m u) -> p g m u", g=2, u=2)
+            src = t[:].rearrange("p (g u) m -> p g m u", u=2)
+            if eng == "v":
+                nc.vector.tensor_copy(out=dst, in_=src)
+            else:
+                nc.scalar.copy(out=dst, in_=src)
+
+        def quant_x(i, part, parts):
+            if i not in x_codes:
+                ct = work.tile([P, G, P], U32, name="x_codes", align_bytes=64)
+                st = work.tile([P, G, P], U8, name="x_scales", align_bytes=64)
+                x_codes[i], x_scales[i] = ct, st
+            gg = slice(part * G // parts, (part + 1) * G // parts)
+            nc.vector.quantize_mx(
+                out=x_codes[i][:, gg, :].rearrange("p g m -> p (g m)").bitcast(FP8X4),
+                scales=x_scales[i][:, gg, :].rearrange("p g m -> p (g m)"),
+                in_=x_group[i][:, gg, :, :].rearrange("p g m t -> p (g m t)"),
+            )
+
+        def transpose_y(pair, b):
+            t = bank(b, [P, 4, P], F32)
+            for s in range(4):
+                i, u = 2 * pair + s // 2, s % 2
+                src = y_raw[:, i, :].bitcast(F32)[:, u : L // 2 : 2]
+                nc.tensor.transpose(t[:, s, :], src, ident_f[:])
+            return t
+
+        def stress_y(pair, t):
+            gt = work.tile([P, 2, P, 4], BF16, name="y_group", align_bytes=64)
+            y_group[pair] = gt
+            src = t[:].rearrange("p s m -> p (s m)").bitcast(BF16)
+            src = src.rearrange("p (j u m e) -> p j m u e", j=2, u=2, e=2)
+            fac = stress_col[:].rearrange("p (o u e) -> p o u e", o=1, u=2).to_broadcast([P, P, 2, 2])
+            for j in range(2):
+                nc.vector.tensor_tensor(
+                    out=gt[:, j, :, :].rearrange("p m (u e) -> p m u e", u=2),
+                    in0=src[:, j],
+                    in1=fac,
+                    op=MULT,
+                )
+
+        def quant_y(pair):
+            ct = work.tile([P, 2, P], U32, name="y_codes", align_bytes=64)
+            st = work.tile([P, 2, P], U8, name="y_scales", align_bytes=64)
+            y_codes[pair], y_scales[pair] = ct, st
+            nc.vector.quantize_mx(
+                out=ct[:].rearrange("p j m -> p (j m)").bitcast(FP8X4),
+                scales=st[:].rearrange("p j m -> p (j m)"),
+                in_=y_group[pair][:].rearrange("p j m t -> p (j m t)"),
+            )
+
+        def group_d(n, eng):
+            src = d_raw[n][:].rearrange("p j n -> p n j")
+            if eng == "v":
+                nc.vector.tensor_copy(out=d_grouped[n][:], in_=src)
+            else:
+                nc.scalar.copy(out=d_grouped[n][:], in_=src)
+
+        def quant_d(n):
+            nc.vector.quantize_mx(
+                out=d_codes[n][:].bitcast(FP8X4),
+                scales=d_scales[n][:],
+                in_=d_grouped[n][:].rearrange("p n j -> p (n j)"),
+            )
+
+        acc = {}
+
+        def mm_x(i, n, g, b):
+            if g == 0:
+                acc[i, n] = bank(b, [P, NB], F32)
+            nc.tensor.matmul_mx(
+                out=acc[i, n][:],
+                lhsT=x_codes[i][:, g, :].bitcast(FP8X4),
+                lhsT_scale=x_scales[i][:, g, :],
+                rhs=words[:, g, 2 * NB * n : 2 * NB * (n + 1)].bitcast(FP4X4),
+                rhs_scale=scales[g][:, NB * n : NB * (n + 1)],
+                start=(g == 0),
+                stop=False,
+            )
+
+        def mm_y(i, n):
+            nc.tensor.matmul_mx(
+                out=acc[i, n][:],
+                lhsT=y_codes[i // 2][:, i % 2, :].bitcast(FP8X4),
+                lhsT_scale=y_scales[i // 2][:, i % 2, :],
+                rhs=d_codes[n][:].bitcast(FP8X4),
+                rhs_scale=d_scales[n][:],
+                start=False,
+                stop=True,
+            )
+
+        disc, res = {}, {}
+
+        def discount(i):
+            t = work.tile([P, N], F32, name="disc")
+            disc[i] = t
+            nc.scalar.activation(
+                out=t[:], in_=spread_row[:], func=ACT.Exp, scale=neg_dur[:, i : i + 1]
+            )
+
+        def finish(i, n, parts=1):
+            if i not in res:
+                rt = work.tile([P, N], F32, name="res")
+                res[i] = rt
+            w = NB // parts
+            for h in range(parts):
+                c = slice(NB * n + w * h, NB * n + w * (h + 1))
+                nc.vector.tensor_tensor(
+                    out=res[i][:, c], in0=acc[i, n][:, w * h : w * (h + 1)], in1=disc[i][:, c], op=MULT
+                )
+                if i == TILES - 1:
+                    nc.sync.dma_start(out=out_view[:, i, c], in_=res[i][:, c])
+
+        def store(i):
+            nc.sync.dma_start(out=out_view[:, i, :], in_=res[i][:])
+
+        with tc.manual_schedule():
+            load_x(0, 0, 2)
+            load_x(0, 1, 2)
+            nc.vector.memset(warm[:], 0.0)
+            nc.vector.memset(scales_a[:].bitcast(I32), 0)
+            nc.vector.memset(scales_b[:].bitcast(I32), 0)
+            make_identity(nc, ident_f[:])
+            make_identity(nc, ident_b[:])
+            nc.scalar.activation(out=warm[:], in_=warm[:], func=ACT.Exp)
+            load_scales(scales_a, 0, 2)
+            load_words(0)
+            nc.scalar.dma_start(
+                out=spread_col[:], in_=spread.rearrange("(b p c) -> p b c", b=2, c=6)
+            )
+            nc.scalar.dma_start(out=dur_raw[:], in_=duration.rearrange("(p i) -> p i", i=TILES))
+            nc.scalar.dma_start(out=stress_col[:], in_=stress.rearrange("(p t) -> p t", t=4))
+            load_words(1)
+            load_d(0)
+            load_x(1, 0, 1)
+            load_scales(scales_b, 2, G)
+            load_words(2)
+            load_words(3)
+            load_y(0, 2)
+            load_d(1)
+            load_d(2)
+            load_x(2, 0, 1)
+            load_x(3, 0, 1)
+            load_y(2, TILES)
+            for i in range(4, TILES):
+                load_x(i, 0, 1)
+
+            t0 = transpose_x(0, 0, 3)
+            t1 = transpose_x(0, 1, 4)
+            copy_x(0, 0, t0, "s")
+            copy_x(0, 1, t1, "v")
+            quant_x(0, 0, 2)
+            quant_x(0, 1, 2)
+            for b in range(2):
+                t = bank(5 + b, [P, 6, P], BF16)
+                for c in range(6):
+                    nc.tensor.transpose(
+                        t[:, c, :], spread_col[:, b, c : c + 1].to_broadcast([P, P]), ident_b[:]
+                    )
+                nc.vector.tensor_copy(
+                    out=spread_row[:, 768 * b : 768 * (b + 1)].rearrange("p (q c) -> p q c", c=6),
+                    in_=t[:].rearrange("p c q -> p q c"),
+                )
+            nc.vector.tensor_scalar_mul(neg_dur[:], dur_raw[:], -1.0)
+            discount(0)
+            group_d(0, "v")
+            for g in (0, 1):
+                for n in range(NN):
+                    mm_x(0, n, g, n)
+            t0 = transpose_x(1, 0, 3)
+            t1 = transpose_x(1, 1, 4)
+            copy_x(1, 0, t0, "s")
+            quant_d(0)
+            copy_x(1, 1, t1, "v")
+            for g in (2, 3):
+                for n in range(NN):
+                    mm_x(0, n, g, n)
+            quant_x(1, 0, 2)
+            quant_x(1, 1, 2)
+            discount(1)
+            ty = transpose_y(0, 7)
+            stress_y(0, ty)
+            group_d(1, "v")
+            quant_y(0)
+            quant_d(1)
+            group_d(2, "s")
+            for n, b in ((0, 5), (1, 6)):
+                for g in range(G):
+                    mm_x(1, n, g, b)
+            t0 = transpose_x(2, 0, 3)
+            t1 = transpose_x(2, 1, 4)
+            for g in range(G):
+                mm_x(1, 2, g, 7)
+            for n in (0, 1):
+                mm_y(0, n)
+                mm_y(1, n)
+            copy_x(2, 0, t0, "s")
+            copy_x(2, 1, t1, "v")
+            quant_d(2)
+            finish(0, 0)
+            quant_x(2, 0, 1)
+            discount(2)
+            mm_y(0, 2)
+            mm_y(1, 2)
+            finish(0, 1)
+            permute_x(3)
+            for g in range(G):
+                mm_x(2, 0, g, 0)
+            finish(1, 0)
+            t0 = transpose_x(3, 0, 3)
+            t1 = transpose_x(3, 1, 4)
+            ty = transpose_y(1, 5)
+            copy_x(3, 0, t0, "s")
+            copy_x(3, 1, t1, "s")
+            finish(0, 2)
+            store(0)
+            for n in (1, 2):
+                for g in range(G):
+                    mm_x(2, n, g, n)
+            stress_y(1, ty)
+            quant_x(3, 0, 1)
+            quant_y(1)
+            finish(1, 1)
+            finish(1, 2)
+            store(1)
+            permute_x(4)
+            discount(3)
+            for n in range(NN):
+                mm_y(2, n)
+
+            ahead = {3: (4,), 4: (5, 6), 6: (7,)}
+            for i in range(3, TILES):
+                ts = []
+                for j in ahead.get(i, ()):
+                    b = 3 + 2 * (j == 6)
+                    ts.append((j, 0, transpose_x(j, 0, b)))
+                    ts.append((j, 1, transpose_x(j, 1, b + 1)))
+                if i in (3, 4):
+                    pair = i - 1
+                    ty = transpose_y(pair, 7)
+                for j, half, t in ts:
+                    copy_x(j, half, t, "s")
+                if i == 3:
+                    for n in range(NN):
+                        finish(2, n)
+                    store(2)
+                for n in range(NN):
+                    for g in range(G):
+                        mm_x(i, n, g, n)
+                    mm_y(i, n)
+                    if n == 0:
+                        if i in (3, 4):
+                            stress_y(pair, ty)
+                            quant_y(pair)
+                        for j in ahead.get(i, ()):
+                            quant_x(j, 0, 1)
+                    if i == 3 and n < 2:
+                        permute_x(5 + n)
+                    if i == 4 and n == 0:
+                        permute_x(7)
+                    finish(i, n, 2 if (i == TILES - 1 and n == NN - 1) else 1)
+                if i < TILES - 1:
+                    store(i)
+                    discount(i + 1)

@@ -93,7 +93,7 @@ def tile_stressed_rating_migration_s1_kernel(
             nc.sync.dma_start(out=d_raw[n][:], in_=d_view[:, :, n * NB : (n + 1) * NB])
 
         x_perm, x_group, x_codes, x_scales = {}, {}, {}, {}
-        y_group, y_codes, y_scales = {}, {}, {}
+        y_perm, y_group, y_codes, y_scales = {}, {}, {}, {}
 
         def permute_x(i):
             t = work.tile([P, 2, K // 4], F32, name="x_perm", align_bytes=64)
@@ -137,12 +137,16 @@ def tile_stressed_rating_migration_s1_kernel(
                 in_=x_group[i][:, gg, :, :].rearrange("p g m t -> p (g m t)"),
             )
 
+        def permute_y(pair):
+            t = work.tile([P, 2, 2, P], F32, name="y_perm", align_bytes=64)
+            y_perm[pair] = t
+            src = y_raw[:, 2 * pair : 2 * pair + 2, :].rearrange("p j l -> p (j l)").bitcast(F32)
+            nc.scalar.copy(out=t[:], in_=src.rearrange("p (j w u) -> p j u w", j=2, u=2))
+
         def transpose_y(pair, b):
             t = bank(b, [P, 4, P], F32)
             for s in range(4):
-                i, u = 2 * pair + s // 2, s % 2
-                src = y_raw[:, i, :].bitcast(F32)[:, u : L // 2 : 2]
-                nc.tensor.transpose(t[:, s, :], src, ident_f[:])
+                nc.tensor.transpose(t[:, s, :], y_perm[pair][:, s // 2, s % 2, :], ident_f[:])
             return t
 
         def stress_y(pair, t):
@@ -240,25 +244,24 @@ def tile_stressed_rating_migration_s1_kernel(
             nc.vector.memset(warm[:], 0.0)
             nc.vector.memset(scales_a[:].bitcast(I32), 0)
             nc.vector.memset(scales_b[:].bitcast(I32), 0)
+            nc.gpsimd.dma_start(
+                out=spread_col[:], in_=spread.rearrange("(b p c) -> p b c", b=2, c=6)
+            )
             make_identity(nc, ident_f[:])
             make_identity(nc, ident_b[:])
+            nc.gpsimd.dma_start(out=dur_raw[:], in_=duration.rearrange("(p i) -> p i", i=TILES))
+            nc.gpsimd.dma_start(out=stress_col[:], in_=stress.rearrange("(p t) -> p t", t=4))
             nc.scalar.activation(out=warm[:], in_=warm[:], func=ACT.Exp)
             load_scales(scales_a, 0, 2)
             load_words(0)
-            nc.scalar.dma_start(
-                out=spread_col[:], in_=spread.rearrange("(b p c) -> p b c", b=2, c=6)
-            )
-            nc.scalar.dma_start(out=dur_raw[:], in_=duration.rearrange("(p i) -> p i", i=TILES))
-            nc.scalar.dma_start(out=stress_col[:], in_=stress.rearrange("(p t) -> p t", t=4))
             load_words(1)
-            load_d(0)
             load_x(1, 0, 1)
+            load_y(0, 2)
             load_scales(scales_b, 2, G)
             load_words(2)
             load_words(3)
-            load_y(0, 2)
-            load_d(1)
-            load_d(2)
+            for n in range(NN):
+                load_d(n)
             load_x(2, 0, 1)
             load_x(3, 0, 1)
             load_y(2, TILES)
@@ -268,65 +271,67 @@ def tile_stressed_rating_migration_s1_kernel(
             t0 = transpose_x(0, 0, 3)
             t1 = transpose_x(0, 1, 4)
             copy_x(0, 0, t0, "s")
-            copy_x(0, 1, t1, "v")
             quant_x(0, 0, 2)
-            quant_x(0, 1, 2)
+            copy_x(0, 1, t1, "v")
+            spread_banks = []
             for b in range(2):
                 t = bank(5 + b, [P, 6, P], BF16)
+                spread_banks.append(t)
                 for c in range(6):
                     nc.tensor.transpose(
                         t[:, c, :], spread_col[:, b, c : c + 1].to_broadcast([P, P]), ident_b[:]
                     )
+            quant_x(0, 1, 2)
+            for b in range(2):
                 nc.vector.tensor_copy(
                     out=spread_row[:, 768 * b : 768 * (b + 1)].rearrange("p (q c) -> p q c", c=6),
-                    in_=t[:].rearrange("p c q -> p q c"),
+                    in_=spread_banks[b][:].rearrange("p c q -> p q c"),
                 )
-            nc.vector.tensor_scalar_mul(neg_dur[:], dur_raw[:], -1.0)
-            discount(0)
-            group_d(0, "v")
             for g in (0, 1):
                 for n in range(NN):
                     mm_x(0, n, g, n)
+            permute_x(1)
+            permute_y(0)
+            nc.vector.tensor_scalar_mul(neg_dur[:], dur_raw[:], -1.0)
             t0 = transpose_x(1, 0, 3)
             t1 = transpose_x(1, 1, 4)
+            ty = transpose_y(0, 7)
             copy_x(1, 0, t0, "s")
-            quant_d(0)
-            copy_x(1, 1, t1, "v")
+            copy_x(1, 1, t1, "s")
+            stress_y(0, ty)
+            quant_x(1, 0, 1)
+            quant_y(0)
             for g in (2, 3):
                 for n in range(NN):
                     mm_x(0, n, g, n)
-            quant_x(1, 0, 2)
-            quant_x(1, 1, 2)
-            discount(1)
-            ty = transpose_y(0, 7)
-            stress_y(0, ty)
-            group_d(1, "v")
-            quant_y(0)
-            quant_d(1)
-            group_d(2, "s")
-            for n, b in ((0, 5), (1, 6)):
+            discount(0)
+            group_d(0, "v")
+            group_d(1, "s")
+            quant_d(0)
+            group_d(2, "v")
+            for n, b in ((0, 5), (1, 6), (2, 7)):
                 for g in range(G):
                     mm_x(1, n, g, b)
+            quant_d(2)
+            quant_d(1)
+            mm_y(0, 0)
+            mm_y(1, 0)
             t0 = transpose_x(2, 0, 3)
             t1 = transpose_x(2, 1, 4)
-            for g in range(G):
-                mm_x(1, 2, g, 7)
-            for n in (0, 1):
+            copy_x(2, 0, t0, "s")
+            copy_x(2, 1, t1, "s")
+            discount(1)
+            permute_y(1)
+            for n in (1, 2):
                 mm_y(0, n)
                 mm_y(1, n)
-            copy_x(2, 0, t0, "s")
-            copy_x(2, 1, t1, "v")
-            quant_d(2)
             finish(0, 0)
             quant_x(2, 0, 1)
-            discount(2)
-            mm_y(0, 2)
-            mm_y(1, 2)
-            finish(0, 1)
             permute_x(3)
+            finish(0, 1)
+            finish(1, 0)
             for g in range(G):
                 mm_x(2, 0, g, 0)
-            finish(1, 0)
             t0 = transpose_x(3, 0, 3)
             t1 = transpose_x(3, 1, 4)
             ty = transpose_y(1, 5)
@@ -334,16 +339,19 @@ def tile_stressed_rating_migration_s1_kernel(
             copy_x(3, 1, t1, "s")
             finish(0, 2)
             store(0)
+            discount(2)
+            permute_y(2)
+            permute_y(3)
             for n in (1, 2):
                 for g in range(G):
                     mm_x(2, n, g, n)
             stress_y(1, ty)
             quant_x(3, 0, 1)
+            permute_x(4)
             quant_y(1)
             finish(1, 1)
             finish(1, 2)
             store(1)
-            permute_x(4)
             discount(3)
             for n in range(NN):
                 mm_y(2, n)
@@ -355,27 +363,29 @@ def tile_stressed_rating_migration_s1_kernel(
                     b = 3 + 2 * (j == 6)
                     ts.append((j, 0, transpose_x(j, 0, b)))
                     ts.append((j, 1, transpose_x(j, 1, b + 1)))
-                if i in (3, 4):
-                    pair = i - 1
-                    ty = transpose_y(pair, 7)
+                tys = []
+                if i == 3:
+                    tys = [(2, transpose_y(2, 6)), (3, transpose_y(3, 7))]
                 for j, half, t in ts:
                     copy_x(j, half, t, "s")
                 if i == 3:
                     for n in range(NN):
                         finish(2, n)
                     store(2)
+                    permute_x(5)
                 for n in range(NN):
                     for g in range(G):
                         mm_x(i, n, g, n)
                     mm_y(i, n)
                     if n == 0:
-                        if i in (3, 4):
-                            stress_y(pair, ty)
-                            quant_y(pair)
                         for j in ahead.get(i, ()):
                             quant_x(j, 0, 1)
-                    if i == 3 and n < 2:
-                        permute_x(5 + n)
+                        for pair, ty in tys:
+                            stress_y(pair, ty)
+                        for pair, ty in tys:
+                            quant_y(pair)
+                    if i == 3 and n == 0:
+                        permute_x(6)
                     if i == 4 and n == 0:
                         permute_x(7)
                     finish(i, n, 2 if (i == TILES - 1 and n == NN - 1) else 1)

@@ -95,19 +95,20 @@ def tile_stressed_rating_migration_s1_kernel(
         x_perm, x_group, x_codes, x_scales = {}, {}, {}, {}
         y_perm, y_group, y_codes, y_scales = {}, {}, {}, {}
 
-        def permute_x(i):
-            t = work.tile([P, 2, K // 4], F32, name="x_perm", align_bytes=64)
-            nc.vector.tensor_copy(
-                out=t[:], in_=x_raw[i][:].bitcast(F32).rearrange("p (w u) -> p u w", u=2)
-            )
-            x_perm[i] = t
+        def permute_x(i, halves=(0, 1)):
+            if i not in x_perm:
+                t = work.tile([P, 2, 2, K // 8], F32, name="x_perm", align_bytes=64)
+                x_perm[i] = t
+            h = slice(halves[0], halves[-1] + 1)
+            src = x_raw[i][:].bitcast(F32).rearrange("p (h w u) -> p h u w", h=2, u=2)
+            nc.vector.tensor_copy(out=x_perm[i][:, h, :, :], in_=src[:, h, :, :])
 
         def transpose_x(i, half, b):
             t = bank(b, [P, 4, P], F32)
             for s in range(4):
                 g, u = 2 * half + s // 2, s % 2
-                if i in x_perm:
-                    src = x_perm[i][:, u, P * g : P * (g + 1)]
+                if i in x_perm and (i, half) != (0, 0):
+                    src = x_perm[i][:, half, u, P * (s // 2) : P * (s // 2 + 1)]
                 else:
                     src = x_raw[i][:].bitcast(F32)[:, 256 * g + u : 256 * (g + 1) : 2]
                 nc.tensor.transpose(t[:, s, :], src, ident_f[:])
@@ -240,48 +241,47 @@ def tile_stressed_rating_migration_s1_kernel(
 
         with tc.manual_schedule():
             load_x(0, 0, 2)
-            load_x(0, 1, 2)
+            nc.scalar.dma_start(
+                out=spread_col[:], in_=spread.rearrange("(b p c) -> p b c", b=2, c=6)
+            )
             nc.vector.memset(warm[:], 0.0)
             nc.vector.memset(scales_a[:].bitcast(I32), 0)
             nc.vector.memset(scales_b[:].bitcast(I32), 0)
-            nc.gpsimd.dma_start(
-                out=spread_col[:], in_=spread.rearrange("(b p c) -> p b c", b=2, c=6)
-            )
             make_identity(nc, ident_f[:])
             make_identity(nc, ident_b[:])
-            nc.gpsimd.dma_start(out=dur_raw[:], in_=duration.rearrange("(p i) -> p i", i=TILES))
-            nc.gpsimd.dma_start(out=stress_col[:], in_=stress.rearrange("(p t) -> p t", t=4))
             nc.scalar.activation(out=warm[:], in_=warm[:], func=ACT.Exp)
             load_scales(scales_a, 0, 2)
             load_words(0)
             load_words(1)
-            load_x(1, 0, 1)
+            load_x(1, 0, 2)
+            load_x(0, 1, 2)
+            load_x(1, 1, 2)
+            nc.sync.dma_start(out=dur_raw[:], in_=duration.rearrange("(p i) -> p i", i=TILES))
+            nc.sync.dma_start(out=stress_col[:], in_=stress.rearrange("(p t) -> p t", t=4))
             load_y(0, 2)
             load_scales(scales_b, 2, G)
             load_words(2)
             load_words(3)
-            for n in range(NN):
-                load_d(n)
+            load_d(0)
             load_x(2, 0, 1)
+            load_d(1)
+            load_d(2)
             load_x(3, 0, 1)
             load_y(2, TILES)
             for i in range(4, TILES):
                 load_x(i, 0, 1)
 
             t0 = transpose_x(0, 0, 3)
-            t1 = transpose_x(0, 1, 4)
             copy_x(0, 0, t0, "s")
             quant_x(0, 0, 2)
-            copy_x(0, 1, t1, "v")
             spread_banks = []
             for b in range(2):
-                t = bank(5 + b, [P, 6, P], BF16)
+                t = bank(6 + b, [P, 6, P], BF16)
                 spread_banks.append(t)
                 for c in range(6):
                     nc.tensor.transpose(
                         t[:, c, :], spread_col[:, b, c : c + 1].to_broadcast([P, P]), ident_b[:]
                     )
-            quant_x(0, 1, 2)
             for b in range(2):
                 nc.vector.tensor_copy(
                     out=spread_row[:, 768 * b : 768 * (b + 1)].rearrange("p (q c) -> p q c", c=6),
@@ -290,39 +290,49 @@ def tile_stressed_rating_migration_s1_kernel(
             for g in (0, 1):
                 for n in range(NN):
                     mm_x(0, n, g, n)
-            permute_x(1)
-            permute_y(0)
             nc.vector.tensor_scalar_mul(neg_dur[:], dur_raw[:], -1.0)
+            permute_x(1, (0,))
+            permute_x(0, (1,))
+            permute_x(1, (1,))
+            permute_y(0)
             t0 = transpose_x(1, 0, 3)
-            t1 = transpose_x(1, 1, 4)
-            ty = transpose_y(0, 7)
+            t1 = transpose_x(0, 1, 4)
+            t2 = transpose_x(1, 1, 5)
+            ty = transpose_y(0, 6)
             copy_x(1, 0, t0, "s")
-            copy_x(1, 1, t1, "s")
+            copy_x(1, 1, t2, "s")
+            quant_x(1, 0, 2)
+            copy_x(0, 1, t1, "v")
+            quant_x(1, 1, 2)
+            quant_x(0, 1, 2)
             stress_y(0, ty)
-            quant_x(1, 0, 1)
             quant_y(0)
+            for g in (0, 1):
+                for n in range(NN):
+                    mm_x(1, n, g, (7, 5, 3)[n])
             for g in (2, 3):
                 for n in range(NN):
                     mm_x(0, n, g, n)
+            for n in range(NN):
+                mm_x(1, n, 2, None)
             discount(0)
             group_d(0, "v")
             group_d(1, "s")
             quant_d(0)
             group_d(2, "v")
-            for n, b in ((0, 5), (1, 6), (2, 7)):
-                for g in range(G):
-                    mm_x(1, n, g, b)
             quant_d(2)
             quant_d(1)
+            t0 = transpose_x(2, 0, 4)
+            t1 = transpose_x(2, 1, 6)
+            for n in range(NN):
+                mm_x(1, n, 3, None)
             mm_y(0, 0)
             mm_y(1, 0)
-            t0 = transpose_x(2, 0, 3)
-            t1 = transpose_x(2, 1, 4)
             copy_x(2, 0, t0, "s")
             copy_x(2, 1, t1, "s")
             discount(1)
             permute_y(1)
-            for n in (1, 2):
+            for n in (2, 1):
                 mm_y(0, n)
                 mm_y(1, n)
             finish(0, 0)
@@ -332,9 +342,9 @@ def tile_stressed_rating_migration_s1_kernel(
             finish(1, 0)
             for g in range(G):
                 mm_x(2, 0, g, 0)
-            t0 = transpose_x(3, 0, 3)
-            t1 = transpose_x(3, 1, 4)
-            ty = transpose_y(1, 5)
+            t0 = transpose_x(3, 0, 4)
+            t1 = transpose_x(3, 1, 6)
+            ty = transpose_y(1, 7)
             copy_x(3, 0, t0, "s")
             copy_x(3, 1, t1, "s")
             finish(0, 2)
@@ -360,12 +370,12 @@ def tile_stressed_rating_migration_s1_kernel(
             for i in range(3, TILES):
                 ts = []
                 for j in ahead.get(i, ()):
-                    b = 3 + 2 * (j == 6)
+                    b, b2 = {4: (4, 6), 5: (3, 4), 6: (5, 6), 7: (3, 4)}[j]
                     ts.append((j, 0, transpose_x(j, 0, b)))
-                    ts.append((j, 1, transpose_x(j, 1, b + 1)))
+                    ts.append((j, 1, transpose_x(j, 1, b2)))
                 tys = []
                 if i == 3:
-                    tys = [(2, transpose_y(2, 6)), (3, transpose_y(3, 7))]
+                    tys = [(2, transpose_y(2, 7)), (3, transpose_y(3, 5))]
                 for j, half, t in ts:
                     copy_x(j, half, t, "s")
                 if i == 3:

@@ -138,11 +138,15 @@ def tile_stressed_rating_migration_s1_kernel(
                 in_=x_group[i][:, gg, :, :].rearrange("p g m t -> p (g m t)"),
             )
 
-        def permute_y(pair):
+        def permute_y(pair, eng):
             t = work.tile([P, 2, 2, P], F32, name="y_perm", align_bytes=64)
             y_perm[pair] = t
             src = y_raw[:, 2 * pair : 2 * pair + 2, :].rearrange("p j l -> p (j l)").bitcast(F32)
-            nc.scalar.copy(out=t[:], in_=src.rearrange("p (j w u) -> p j u w", j=2, u=2))
+            src = src.rearrange("p (j w u) -> p j u w", j=2, u=2)
+            if eng == "v":
+                nc.vector.tensor_copy(out=t[:], in_=src)
+            else:
+                nc.scalar.copy(out=t[:], in_=src)
 
         def transpose_y(pair, b):
             t = bank(b, [P, 4, P], F32)
@@ -175,11 +179,12 @@ def tile_stressed_rating_migration_s1_kernel(
             )
 
         def group_d(n, eng):
-            src = d_raw[n][:].rearrange("p j n -> p n j")
+            src = d_raw[n][:].rearrange("p j (c i) -> p c j i", i=4)
+            dst = d_grouped[n][:].rearrange("p (c i) j -> p c j i", i=4)
             if eng == "v":
-                nc.vector.tensor_copy(out=d_grouped[n][:], in_=src)
+                nc.vector.tensor_copy(out=dst, in_=src)
             else:
-                nc.scalar.copy(out=d_grouped[n][:], in_=src)
+                nc.scalar.copy(out=dst, in_=src)
 
         def quant_d(n):
             nc.vector.quantize_mx(
@@ -190,26 +195,27 @@ def tile_stressed_rating_migration_s1_kernel(
 
         acc = {}
 
-        def mm_x(i, n, g, b):
-            if g == 0:
+        def mm_x(i, n, g, b, c0=0, c1=NB):
+            if g == 0 and c0 == 0:
                 acc[i, n] = bank(b, [P, NB], F32)
+            a0, a1 = NB * n + c0, NB * n + c1
             nc.tensor.matmul_mx(
-                out=acc[i, n][:],
+                out=acc[i, n][:, c0:c1],
                 lhsT=x_codes[i][:, g, :].bitcast(FP8X4),
                 lhsT_scale=x_scales[i][:, g, :],
-                rhs=words[:, g, 2 * NB * n : 2 * NB * (n + 1)].bitcast(FP4X4),
-                rhs_scale=scales[g][:, NB * n : NB * (n + 1)],
+                rhs=words[:, g, 2 * a0 : 2 * a1].bitcast(FP4X4),
+                rhs_scale=scales[g][:, a0:a1],
                 start=(g == 0),
                 stop=False,
             )
 
-        def mm_y(i, n):
+        def mm_y(i, n, c0=0, c1=NB):
             nc.tensor.matmul_mx(
-                out=acc[i, n][:],
+                out=acc[i, n][:, c0:c1],
                 lhsT=y_codes[i // 2][:, i % 2, :].bitcast(FP8X4),
                 lhsT_scale=y_scales[i // 2][:, i % 2, :],
-                rhs=d_codes[n][:].bitcast(FP8X4),
-                rhs_scale=d_scales[n][:],
+                rhs=d_codes[n][:, c0:c1].bitcast(FP8X4),
+                rhs_scale=d_scales[n][:, c0:c1],
                 start=False,
                 stop=True,
             )
@@ -217,27 +223,23 @@ def tile_stressed_rating_migration_s1_kernel(
         disc, res = {}, {}
 
         def discount(i):
-            t = work.tile([P, N], F32, name="disc")
+            t = work.tile([P, N], F32, name="disc", bufs=4)
             disc[i] = t
             nc.scalar.activation(
                 out=t[:], in_=spread_row[:], func=ACT.Exp, scale=neg_dur[:, i : i + 1]
             )
 
-        def finish(i, n, parts=1):
+        def finish(i, n, c0=0, c1=NB):
             if i not in res:
                 rt = work.tile([P, N], F32, name="res")
                 res[i] = rt
-            w = NB // parts
-            for h in range(parts):
-                c = slice(NB * n + w * h, NB * n + w * (h + 1))
-                nc.vector.tensor_tensor(
-                    out=res[i][:, c], in0=acc[i, n][:, w * h : w * (h + 1)], in1=disc[i][:, c], op=MULT
-                )
-                if i == TILES - 1:
-                    nc.sync.dma_start(out=out_view[:, i, c], in_=res[i][:, c])
+            c = slice(NB * n + c0, NB * n + c1)
+            nc.vector.tensor_tensor(
+                out=res[i][:, c], in0=acc[i, n][:, c0:c1], in1=disc[i][:, c], op=MULT
+            )
 
-        def store(i):
-            nc.sync.dma_start(out=out_view[:, i, :], in_=res[i][:])
+        def store(i, a0=0, a1=N):
+            nc.sync.dma_start(out=out_view[:, i, a0:a1], in_=res[i][:, a0:a1])
 
         with tc.manual_schedule():
             load_x(0, 0, 2)
@@ -259,16 +261,18 @@ def tile_stressed_rating_migration_s1_kernel(
             nc.sync.dma_start(out=dur_raw[:], in_=duration.rearrange("(p i) -> p i", i=TILES))
             nc.sync.dma_start(out=stress_col[:], in_=stress.rearrange("(p t) -> p t", t=4))
             load_y(0, 2)
+            load_d(0)
             load_scales(scales_b, 2, G)
             load_words(2)
             load_words(3)
-            load_d(0)
             load_x(2, 0, 1)
             load_d(1)
             load_d(2)
+            load_y(2, 4)
             load_x(3, 0, 1)
-            load_y(2, TILES)
-            for i in range(4, TILES):
+            load_x(4, 0, 1)
+            load_y(4, TILES)
+            for i in range(5, TILES):
                 load_x(i, 0, 1)
 
             t0 = transpose_x(0, 0, 3)
@@ -294,7 +298,7 @@ def tile_stressed_rating_migration_s1_kernel(
             permute_x(1, (0,))
             permute_x(0, (1,))
             permute_x(1, (1,))
-            permute_y(0)
+            permute_y(0, "v")
             t0 = transpose_x(1, 0, 3)
             t1 = transpose_x(0, 1, 4)
             t2 = transpose_x(1, 1, 5)
@@ -307,6 +311,11 @@ def tile_stressed_rating_migration_s1_kernel(
             quant_x(0, 1, 2)
             stress_y(0, ty)
             quant_y(0)
+            discount(0)
+            discount(1)
+            discount(2)
+            group_d(0, "v")
+            quant_d(0)
             for g in (0, 1):
                 for n in range(NN):
                     mm_x(1, n, g, (7, 5, 3)[n])
@@ -315,67 +324,61 @@ def tile_stressed_rating_migration_s1_kernel(
                     mm_x(0, n, g, n)
             for n in range(NN):
                 mm_x(1, n, 2, None)
-            discount(0)
-            group_d(0, "v")
-            group_d(1, "s")
-            quant_d(0)
-            group_d(2, "v")
-            quant_d(2)
-            quant_d(1)
             t0 = transpose_x(2, 0, 4)
             t1 = transpose_x(2, 1, 6)
-            for n in range(NN):
-                mm_x(1, n, 3, None)
-            mm_y(0, 0)
-            mm_y(1, 0)
             copy_x(2, 0, t0, "s")
             copy_x(2, 1, t1, "s")
-            discount(1)
-            permute_y(1)
-            for n in (2, 1):
+            group_d(1, "v")
+            group_d(2, "s")
+            quant_d(1)
+            quant_x(2, 0, 1)
+            for n in range(NN):
+                mm_x(1, n, 3, None)
+            for n in (0, 1):
                 mm_y(0, n)
                 mm_y(1, n)
+            for n, b in ((0, 4), (1, 6)):
+                for g in range(G):
+                    mm_x(2, n, g, b)
             finish(0, 0)
-            quant_x(2, 0, 1)
-            permute_x(3)
-            finish(0, 1)
             finish(1, 0)
-            for g in range(G):
-                mm_x(2, 0, g, 0)
-            t0 = transpose_x(3, 0, 4)
-            t1 = transpose_x(3, 1, 6)
-            ty = transpose_y(1, 7)
+            permute_x(3)
+            permute_y(1, "s")
+            quant_d(2)
+            finish(0, 1)
+            t0 = transpose_x(3, 0, 0)
+            t1 = transpose_x(3, 1, 7)
+            ty = transpose_y(1, 1)
             copy_x(3, 0, t0, "s")
             copy_x(3, 1, t1, "s")
-            finish(0, 2)
-            store(0)
-            discount(2)
-            permute_y(2)
-            permute_y(3)
-            for n in (1, 2):
-                for g in range(G):
-                    mm_x(2, n, g, n)
+            mm_y(0, 2)
+            mm_y(1, 2)
+            finish(1, 1)
+            for g in range(G):
+                mm_x(2, 2, g, 5)
             stress_y(1, ty)
+            quant_y(1)
             quant_x(3, 0, 1)
             permute_x(4)
-            quant_y(1)
-            finish(1, 1)
+            finish(0, 2)
+            store(0)
             finish(1, 2)
             store(1)
+            permute_y(2, "s")
             discount(3)
             for n in range(NN):
                 mm_y(2, n)
 
-            ahead = {3: (4,), 4: (5, 6), 6: (7,)}
+            ahead = {3: (4,), 4: (5, 6), 5: (7,)}
             for i in range(3, TILES):
                 ts = []
                 for j in ahead.get(i, ()):
-                    b, b2 = {4: (4, 6), 5: (3, 4), 6: (5, 6), 7: (3, 4)}[j]
+                    b, b2 = (5, 6) if j == 6 else (0, 7)
                     ts.append((j, 0, transpose_x(j, 0, b)))
                     ts.append((j, 1, transpose_x(j, 1, b2)))
-                tys = []
-                if i == 3:
-                    tys = [(2, transpose_y(2, 7)), (3, transpose_y(3, 5))]
+                if i in (3, 5):
+                    pair = (i + 1) // 2
+                    ty = transpose_y(pair, 1)
                 for j, half, t in ts:
                     copy_x(j, half, t, "s")
                 if i == 3:
@@ -384,21 +387,28 @@ def tile_stressed_rating_migration_s1_kernel(
                     store(2)
                     permute_x(5)
                 for n in range(NN):
-                    for g in range(G):
-                        mm_x(i, n, g, n)
-                    mm_y(i, n)
+                    last = i == TILES - 1 and n == NN - 1
+                    w = P if last else NB
+                    for c0 in range(0, NB, w):
+                        for g in range(G):
+                            mm_x(i, n, g, n + 2, c0, c0 + w)
+                        mm_y(i, n, c0, c0 + w)
                     if n == 0:
                         for j in ahead.get(i, ()):
                             quant_x(j, 0, 1)
-                        for pair, ty in tys:
+                        if i in (3, 5):
                             stress_y(pair, ty)
-                        for pair, ty in tys:
                             quant_y(pair)
                     if i == 3 and n == 0:
                         permute_x(6)
                     if i == 4 and n == 0:
                         permute_x(7)
-                    finish(i, n, 2 if (i == TILES - 1 and n == NN - 1) else 1)
+                    for c0 in range(0, NB, w):
+                        finish(i, n, c0, c0 + w)
+                        if i == TILES - 1:
+                            store(i, NB * n + c0, NB * n + c0 + w)
                 if i < TILES - 1:
                     store(i)
                     discount(i + 1)
+                if i == 3:
+                    permute_y(3, "s")

from contextlib import ExitStack

import concourse.mybir as mybir
from concourse.masks import make_identity

M, K, L, N = 1024, 2048, 512, 1536
FLOPS = 2 * M * (K + L) * N

F32 = mybir.dt.float32
BF16 = mybir.dt.bfloat16
U32 = mybir.dt.uint32
I32 = mybir.dt.int32
U8 = mybir.dt.uint8
FP8X4 = mybir.dt.float8_e4m3fn_x4
FP4X4 = mybir.dt.float4_e2m1fn_x4
ACT = mybir.ActivationFunctionType
MULT = mybir.AluOpType.mult

P = 128
TILES = M // P
G = K // 512
NB = 512
NN = N // NB


def tile_stressed_rating_migration_s1_kernel(
    tc, x, y, stress, base_words, base_scales, distressed, duration, spread, out
):
    nc = tc.nc
    with ExitStack() as ctx:
        keep = ctx.enter_context(tc.tile_pool(name="keep", bufs=1))
        work = ctx.enter_context(tc.tile_pool(name="work", bufs=3))
        psum = ctx.enter_context(tc.psum_pool(name="psum", bufs=1))

        x_view = x.rearrange("(p i) k -> p i k", i=TILES)
        y_view = y.rearrange("(p i) l -> p i l", i=TILES)
        out_view = out.rearrange("(p i) n -> p i n", i=TILES)

        def bank(b, shape, dtype):
            t = psum.tile(shape, dtype, name=f"bank{b}", tag=f"bank{b}")
            return t

        x_raw = []
        for i in range(TILES):
            t = keep.tile([P, K], BF16, name=f"x_raw{i}", align_bytes=64)
            x_raw.append(t)
        y_raw = keep.tile([P, TILES, L], BF16, name="y_raw", align_bytes=64)
        words = keep.tile([P, G, 2 * N], U8, name="words", align_bytes=64)
        scales_a = keep.tile([P, 2, N], U8, name="scales_a", align_bytes=64)
        scales_b = keep.tile([P, 2, N], U8, name="scales_b", align_bytes=64)
        scales = [scales_a[:, 0, :], scales_a[:, 1, :], scales_b[:, 0, :], scales_b[:, 1, :]]
        d_raw, d_grouped, d_codes, d_scales = [], [], [], []
        for n in range(NN):
            t = keep.tile([P, 4, NB], BF16, name=f"d_raw{n}", align_bytes=64)
            d_raw.append(t)
            t = keep.tile([P, NB, 4], BF16, name=f"d_grouped{n}", align_bytes=64)
            d_grouped.append(t)
            t = keep.tile([P, NB], U32, name=f"d_codes{n}", align_bytes=64)
            d_codes.append(t)
            t = keep.tile([P, NB], U8, name=f"d_scales{n}", align_bytes=64)
            d_scales.append(t)
        spread_col = keep.tile([P, 2, 6], BF16, name="spread_col")
        spread_row = keep.tile([P, N], BF16, name="spread_row")
        stress_col = keep.tile([P, 4], BF16, name="stress_col")
        dur_raw = keep.tile([P, TILES], BF16, name="dur_raw")
        neg_dur = keep.tile([P, TILES], F32, name="neg_dur")
        ident_f = keep.tile([P, P], F32, name="ident_f")
        ident_b = keep.tile([P, P], BF16, name="ident_b")
        warm = keep.tile([P, 1], F32, name="warm")

        def load_x(i, part, parts):
            w = K // parts
            nc.sync.dma_start(
                out=x_raw[i][:, part * w : (part + 1) * w],
                in_=x_view[:, i, part * w : (part + 1) * w],
            )

        def load_y(i0, i1):
            nc.sync.dma_start(out=y_raw[:, i0:i1, :], in_=y_view[:, i0:i1, :])

        def load_words(g):
            nc.sync.dma_start(out=words[:, g, :].bitcast(I32), in_=base_words[g].bitcast(I32))

        def load_scales(t, g0, g1):
            for q in range(4):
                nc.sync.dma_start(
                    out=t[32 * q : 32 * q + 4, :, :].bitcast(I32),
                    in_=base_scales[g0:g1, 4 * q : 4 * q + 4, :].rearrange("g r n -> r g n").bitcast(I32),
                )

        def load_d(n):
            d_view = distressed.rearrange("(p j) n -> p j n", j=4)
            nc.sync.dma_start(out=d_raw[n][:], in_=d_view[:, :, n * NB : (n + 1) * NB])

        x_perm, x_group, x_codes, x_scales = {}, {}, {}, {}
        y_perm, y_group, y_codes, y_scales = {}, {}, {}, {}

        def permute_x(i, halves=(0, 1)):
            if i not in x_perm:
                t = work.tile([P, 2, 2, K // 8], F32, name="x_perm", align_bytes=64)
                x_perm[i] = t
            h = slice(halves[0], halves[-1] + 1)
            src = x_raw[i][:].bitcast(F32).rearrange("p (h w u) -> p h u w", h=2, u=2)
            nc.vector.tensor_copy(out=x_perm[i][:, h, :, :], in_=src[:, h, :, :])

        def transpose_x(i, half, b):
            t = bank(b, [P, 4, P], F32)
            for s in range(4):
                g, u = 2 * half + s // 2, s % 2
                if i in x_perm and (i, half) != (0, 0):
                    src = x_perm[i][:, half, u, P * (s // 2) : P * (s // 2 + 1)]
                else:
                    src = x_raw[i][:].bitcast(F32)[:, 256 * g + u : 256 * (g + 1) : 2]
                nc.tensor.transpose(t[:, s, :], src, ident_f[:])
            return t

        def copy_x(i, half, t, eng):
            if i not in x_group:
                gt = work.tile([P, G, P, 4], BF16, name="x_group", align_bytes=64)
                x_group[i] = gt
            dst = x_group[i][:, 2 * half : 2 * half + 2, :, :].rearrange("p g m t -> p (g m t)")
            dst = dst.bitcast(F32).rearrange("p (g m u) -> p g m u", g=2, u=2)
            src = t[:].rearrange("p (g u) m -> p g m u", u=2)
            if eng == "v":
                nc.vector.tensor_copy(out=dst, in_=src)
            else:
                nc.scalar.copy(out=dst, in_=src)

        def quant_x(i, part, parts):
            if i not in x_codes:
                ct = work.tile([P, G, P], U32, name="x_codes", align_bytes=64)
                st = work.tile([P, G, P], U8, name="x_scales", align_bytes=64)
                x_codes[i], x_scales[i] = ct, st
            gg = slice(part * G // parts, (part + 1) * G // parts)
            nc.vector.quantize_mx(
                out=x_codes[i][:, gg, :].rearrange("p g m -> p (g m)").bitcast(FP8X4),
                scales=x_scales[i][:, gg, :].rearrange("p g m -> p (g m)"),
                in_=x_group[i][:, gg, :, :].rearrange("p g m t -> p (g m t)"),
            )

        def permute_y(pair, eng):
            t = work.tile([P, 2, 2, P], F32, name="y_perm", align_bytes=64)
            y_perm[pair] = t
            src = y_raw[:, 2 * pair : 2 * pair + 2, :].rearrange("p j l -> p (j l)").bitcast(F32)
            src = src.rearrange("p (j w u) -> p j u w", j=2, u=2)
            if eng == "v":
                nc.vector.tensor_copy(out=t[:], in_=src)
            else:
                nc.scalar.copy(out=t[:], in_=src)

        def transpose_y(pair, b):
            t = bank(b, [P, 4, P], F32)
            for s in range(4):
                nc.tensor.transpose(t[:, s, :], y_perm[pair][:, s // 2, s % 2, :], ident_f[:])
            return t

        def stress_y(pair, t):
            gt = work.tile([P, 2, P, 4], BF16, name="y_group", align_bytes=64)
            y_group[pair] = gt
            src = t[:].rearrange("p s m -> p (s m)").bitcast(BF16)
            src = src.rearrange("p (j u m e) -> p j m u e", j=2, u=2, e=2)
            fac = stress_col[:].rearrange("p (o u e) -> p o u e", o=1, u=2).to_broadcast([P, P, 2, 2])
            for j in range(2):
                nc.vector.tensor_tensor(
                    out=gt[:, j, :, :].rearrange("p m (u e) -> p m u e", u=2),
                    in0=src[:, j],
                    in1=fac,
                    op=MULT,
                )

        def quant_y(pair):
            ct = work.tile([P, 2, P], U32, name="y_codes", align_bytes=64)
            st = work.tile([P, 2, P], U8, name="y_scales", align_bytes=64)
            y_codes[pair], y_scales[pair] = ct, st
            nc.vector.quantize_mx(
                out=ct[:].rearrange("p j m -> p (j m)").bitcast(FP8X4),
                scales=st[:].rearrange("p j m -> p (j m)"),
                in_=y_group[pair][:].rearrange("p j m t -> p (j m t)"),
            )

        def group_d(n, eng):
            src = d_raw[n][:].rearrange("p j (c i) -> p c j i", i=4)
            dst = d_grouped[n][:].rearrange("p (c i) j -> p c j i", i=4)
            if eng == "v":
                nc.vector.tensor_copy(out=dst, in_=src)
            else:
                nc.scalar.copy(out=dst, in_=src)

        def quant_d(n):
            nc.vector.quantize_mx(
                out=d_codes[n][:].bitcast(FP8X4),
                scales=d_scales[n][:],
                in_=d_grouped[n][:].rearrange("p n j -> p (n j)"),
            )

        acc = {}

        def mm_x(i, n, g, b, c0=0, c1=NB):
            if g == 0 and c0 == 0:
                acc[i, n] = bank(b, [P, NB], F32)
            a0, a1 = NB * n + c0, NB * n + c1
            nc.tensor.matmul_mx(
                out=acc[i, n][:, c0:c1],
                lhsT=x_codes[i][:, g, :].bitcast(FP8X4),
                lhsT_scale=x_scales[i][:, g, :],
                rhs=words[:, g, 2 * a0 : 2 * a1].bitcast(FP4X4),
                rhs_scale=scales[g][:, a0:a1],
                start=(g == 0),
                stop=False,
            )

        def mm_y(i, n, c0=0, c1=NB):
            nc.tensor.matmul_mx(
                out=acc[i, n][:, c0:c1],
                lhsT=y_codes[i // 2][:, i % 2, :].bitcast(FP8X4),
                lhsT_scale=y_scales[i // 2][:, i % 2, :],
                rhs=d_codes[n][:, c0:c1].bitcast(FP8X4),
                rhs_scale=d_scales[n][:, c0:c1],
                start=False,
                stop=True,
            )

        disc, res = {}, {}

        def discount(i):
            t = work.tile([P, N], F32, name="disc", bufs=4)
            disc[i] = t
            nc.scalar.activation(
                out=t[:], in_=spread_row[:], func=ACT.Exp, scale=neg_dur[:, i : i + 1]
            )

        def finish(i, n, c0=0, c1=NB):
            if i not in res:
                rt = work.tile([P, N], F32, name="res")
                res[i] = rt
            c = slice(NB * n + c0, NB * n + c1)
            nc.vector.tensor_tensor(
                out=res[i][:, c], in0=acc[i, n][:, c0:c1], in1=disc[i][:, c], op=MULT
            )

        def store(i, a0=0, a1=N):
            nc.sync.dma_start(out=out_view[:, i, a0:a1], in_=res[i][:, a0:a1])

        with tc.manual_schedule():
            load_x(0, 0, 2)
            nc.scalar.dma_start(
                out=spread_col[:], in_=spread.rearrange("(b p c) -> p b c", b=2, c=6)
            )
            nc.vector.memset(warm[:], 0.0)
            nc.vector.memset(scales_a[:].bitcast(I32), 0)
            nc.vector.memset(scales_b[:].bitcast(I32), 0)
            make_identity(nc, ident_f[:])
            make_identity(nc, ident_b[:])
            nc.scalar.activation(out=warm[:], in_=warm[:], func=ACT.Exp)
            load_scales(scales_a, 0, 2)
            load_words(0)
            load_words(1)
            load_x(1, 0, 2)
            load_x(0, 1, 2)
            load_x(1, 1, 2)
            nc.sync.dma_start(out=dur_raw[:], in_=duration.rearrange("(p i) -> p i", i=TILES))
            nc.sync.dma_start(out=stress_col[:], in_=stress.rearrange("(p t) -> p t", t=4))
            load_y(0, 2)
            load_d(0)
            load_scales(scales_b, 2, G)
            load_words(2)
            load_words(3)
            load_x(2, 0, 1)
            load_d(1)
            load_d(2)
            load_y(2, 4)
            load_x(3, 0, 1)
            load_x(4, 0, 1)
            load_y(4, TILES)
            for i in range(5, TILES):
                load_x(i, 0, 1)

            t0 = transpose_x(0, 0, 3)
            copy_x(0, 0, t0, "s")
            quant_x(0, 0, 2)
            spread_banks = []
            for b in range(2):
                t = bank(6 + b, [P, 6, P], BF16)
                spread_banks.append(t)
                for c in range(6):
                    nc.tensor.transpose(
                        t[:, c, :], spread_col[:, b, c : c + 1].to_broadcast([P, P]), ident_b[:]
                    )
            for b in range(2):
                nc.vector.tensor_copy(
                    out=spread_row[:, 768 * b : 768 * (b + 1)].rearrange("p (q c) -> p q c", c=6),
                    in_=spread_banks[b][:].rearrange("p c q -> p q c"),
                )
            for g in (0, 1):
                for n in range(NN):
                    mm_x(0, n, g, n)
            nc.vector.tensor_scalar_mul(neg_dur[:], dur_raw[:], -1.0)
            permute_x(1, (0,))
            permute_x(0, (1,))
            permute_x(1, (1,))
            permute_y(0, "v")
            t0 = transpose_x(1, 0, 3)
            t1 = transpose_x(0, 1, 4)
            t2 = transpose_x(1, 1, 5)
            ty = transpose_y(0, 6)
            copy_x(1, 0, t0, "s")
            copy_x(1, 1, t2, "s")
            quant_x(1, 0, 2)
            copy_x(0, 1, t1, "v")
            quant_x(1, 1, 2)
            quant_x(0, 1, 2)
            stress_y(0, ty)
            quant_y(0)
            discount(0)
            discount(1)
            discount(2)
            group_d(0, "v")
            quant_d(0)
            for g in (0, 1):
                for n in range(NN):
                    mm_x(1, n, g, (7, 5, 3)[n])
            for g in (2, 3):
                for n in range(NN):
                    mm_x(0, n, g, n)
            for n in range(NN):
                mm_x(1, n, 2, None)
            t0 = transpose_x(2, 0, 4)
            t1 = transpose_x(2, 1, 6)
            copy_x(2, 0, t0, "s")
            copy_x(2, 1, t1, "s")
            group_d(1, "v")
            group_d(2, "s")
            quant_d(1)
            quant_x(2, 0, 1)
            for n in range(NN):
                mm_x(1, n, 3, None)
            for n in (0, 1):
                mm_y(0, n)
                mm_y(1, n)
            for n, b in ((0, 4), (1, 6)):
                for g in range(G):
                    mm_x(2, n, g, b)
            finish(0, 0)
            finish(1, 0)
            permute_x(3)
            permute_y(1, "s")
            quant_d(2)
            finish(0, 1)
            t0 = transpose_x(3, 0, 0)
            t1 = transpose_x(3, 1, 7)
            ty = transpose_y(1, 1)
            copy_x(3, 0, t0, "s")
            copy_x(3, 1, t1, "s")
            mm_y(0, 2)
            mm_y(1, 2)
            finish(1, 1)
            for g in range(G):
                mm_x(2, 2, g, 5)
            stress_y(1, ty)
            quant_y(1)
            quant_x(3, 0, 1)
            permute_x(4)
            finish(0, 2)
            store(0)
            finish(1, 2)
            store(1)
            permute_y(2, "s")
            discount(3)
            for n in range(NN):
                mm_y(2, n)

            ahead = {3: (4,), 4: (5, 6), 5: (7,)}
            for i in range(3, TILES):
                ts = []
                for j in ahead.get(i, ()):
                    b, b2 = (5, 6) if j == 6 else (0, 7)
                    ts.append((j, 0, transpose_x(j, 0, b)))
                    ts.append((j, 1, transpose_x(j, 1, b2)))
                if i in (3, 5):
                    pair = (i + 1) // 2
                    ty = transpose_y(pair, 1)
                for j, half, t in ts:
                    copy_x(j, half, t, "s")
                if i == 3:
                    for n in range(NN):
                        finish(2, n)
                    store(2)
                    permute_x(5)
                for n in range(NN):
                    last = i == TILES - 1 and n == NN - 1
                    w = P if last else NB
                    for c0 in range(0, NB, w):
                        for g in range(G):
                            mm_x(i, n, g, n + 2, c0, c0 + w)
                        mm_y(i, n, c0, c0 + w)
                    if n == 0:
                        for j in ahead.get(i, ()):
                            quant_x(j, 0, 1)
                        if i in (3, 5):
                            stress_y(pair, ty)
                            quant_y(pair)
                    if i == 3 and n == 0:
                        permute_x(6)
                    if i == 4 and n == 0:
                        permute_x(7)
                    for c0 in range(0, NB, w):
                        finish(i, n, c0, c0 + w)
                        if i == TILES - 1:
                            store(i, NB * n + c0, NB * n + c0 + w)
                if i < TILES - 1:
                    store(i)
                    discount(i + 1)
                if i == 3:
                    permute_y(3, "s")
